import numpy as np
import ml_dtypes


def mxq(x, axis, fmt="e4m3"):
    dtype, down = {"e4m3": (ml_dtypes.float8_e4m3fn, 7), "e5m2": (ml_dtypes.float8_e5m2, 14)}[fmt]
    v = np.moveaxis(np.asarray(x, np.float32).astype(ml_dtypes.bfloat16).astype(np.float64), axis, -1)
    blocks = v.reshape(v.shape[:-1] + (-1, 32))
    amax = np.abs(blocks).max(-1, keepdims=True)
    byte = np.maximum(np.where(amax > 0, np.frexp(amax)[1] - 1 + 127, 0) - down, 1)
    scale = np.exp2(byte - 127.0)
    codes = (blocks / scale).astype(np.float32).astype(dtype).astype(np.float64)
    return np.moveaxis((codes * scale).reshape(v.shape), -1, axis)


WIDE = False


def mx_kscale(k):
    if not WIDE:
        return np.ones(k)
    levels = np.array([30, -30])
    if k % 512:
        return np.exp2(np.random.permutation(np.resize(levels, k // 32))).repeat(32)
    a = np.empty((k // 512, 16))
    for p in range(k // 512):
        a[p, :8] = np.random.permutation(np.resize(levels, 8))
        for g in range(8):
            far = levels[np.abs(levels - a[p, g]) >= 10]
            a[p, g + 8] = far[np.random.randint(len(far))]
    return np.exp2(a.ravel()).repeat(32)


def f64(x):
    return np.asarray(x).astype(np.float64)


E2M1 = np.array([0.0, 0.5, 1.0, 1.5, 2.0, 3.0, 4.0, 6.0, -0.0, -0.5, -1.0, -1.5, -2.0, -3.0, -4.0, -6.0])


def pack_weight(w, fmt):
    k, n = w.shape
    w = f64(np.asarray(w, np.float32).astype(ml_dtypes.bfloat16)).reshape(k // 32, 32, n)
    amax = np.abs(w).max(1)
    if fmt == "e4m3":
        byte = np.frexp(amax)[1] - 1 + 127 - 7
    else:
        mant, ex = np.frexp(amax / 6.0)
        byte = np.where(mant > 0.5, ex, ex - 1) + 127
    byte = np.clip(np.where(amax > 0, byte, 1), 1, 254)
    scaled = (w * np.exp2(127.0 - byte)[:, None, :]).reshape(k, n).astype(np.float32)
    by_word = np.ascontiguousarray(scaled.reshape(k // 512, 128, 4, n).transpose(0, 1, 3, 2))
    if fmt == "e4m3":
        words = by_word.astype(ml_dtypes.float8_e4m3fn).view(np.uint8)
    else:
        c = by_word.astype(ml_dtypes.float4_e2m1fn).view(np.uint8) & 0xF
        words = (c[..., 0::2] | (c[..., 1::2] << 4)).reshape(k // 512, 128, 2 * n)
    return np.ascontiguousarray(words), np.ascontiguousarray(byte.astype(np.uint8).reshape(k // 512, 16, n))


def unpack_weight(words, scales, fmt):
    g, _, n = scales.shape
    words = np.ascontiguousarray(words).reshape(g, 128, n, -1)
    if fmt == "e4m3":
        vals = words.view(ml_dtypes.float8_e4m3fn).astype(np.float64)
    else:
        nib = np.empty((g, 128, n, 4), np.uint8)
        nib[..., 0::2] = words & 0xF
        nib[..., 1::2] = words >> 4
        vals = E2M1[nib]
    vals = vals * np.repeat(np.exp2(scales.astype(np.float64) - 127.0), 8, axis=1)[..., None]
    return vals.transpose(0, 1, 3, 2).reshape(g * 512, n)


O, K, M, T = 1024, 2560, 512, 512


def setup_inputs():
    n = np.random.standard_normal
    s = mx_kscale(K)[:, None]
    dy = np.exp(0.5 * n((1, T))) * n((K, T))
    w = n((K, M)) / np.sqrt(K) / s
    p_w8 = pack_weight(w[:O], "e4m3")
    p_w4 = pack_weight(w[O:], "e2m1")
    return {
        "dy": (dy * s).astype(np.float32),
        "w8_words": p_w8[0],
        "w8_scales": p_w8[1],
        "w4_words": p_w4[0],
        "w4_scales": p_w4[1],
    }


def reference(dy, w8_words, w8_scales, w4_words, w4_scales):
    dy_ = mxq(f64(dy), 0, "e5m2")
    w8_ = unpack_weight(w8_words, w8_scales, "e4m3")
    w4_ = unpack_weight(w4_words, w4_scales, "e2m1")
    y = dy_[:O].T @ w8_ + dy_[O:].T @ w4_
    return y

@@ -1,0 +1,145 @@
+from contextlib import ExitStack
+
+import concourse.mybir as mybir
+
+K, T, D = 2560, 512, 512
+FLOPS = 2 * K * T * D
+
+F32 = mybir.dt.float32
+BF16 = mybir.dt.bfloat16
+I32 = mybir.dt.int32
+U32 = mybir.dt.uint32
+U8 = mybir.dt.uint8
+E5M2X4 = mybir.dt.float8_e5m2_x4
+E4M3X4 = mybir.dt.float8_e4m3fn_x4
+E2M1X4 = mybir.dt.float4_e2m1fn_x4
+
+P = 128
+J = 4
+PASSES = 5
+W8_PASSES = 2
+W4_PASSES = 3
+BLOCKS = 4
+HALF = T // 2
+V_COLS = 320
+V_HALF = 160
+WHOLE = 3
+HALVES = ((3, 0), (4, 0), (3, 1), (4, 1))
+
+
+def load_scales(nc, plane, scales, passes):
+    rows = scales.bitcast(I32).rearrange("a (q r) d -> r q a d", r=4)
+    for r in range(4):
+        nc.scalar.dma_start(
+            out=plane[r:P:32, :].bitcast(I32).rearrange("q (a d) -> q a d", a=passes), in_=rows[r]
+        )
+
+
+def interleave(copy, grouped, raw, t0, t1):
+    copy(
+        out=grouped[:, t0:t1, :].rearrange("p (c i) j -> p c j i", i=4),
+        in_=raw[:, :, t0:t1].rearrange("p j (c i) -> p c j i", i=4),
+    )
+
+
+def tile_mix_dyq_tm_none_kernel(tc, dy, w8_words, w8_scales, w4_words, w4_scales, out):
+    nc = tc.nc
+    dy_rows = dy.rearrange("(g p j) t -> g p j t", p=P, j=J)
+
+    with ExitStack() as ctx:
+        keep = ctx.enter_context(tc.tile_pool(name="keep", bufs=1))
+        psum = ctx.enter_context(tc.psum_pool(name="psum", bufs=1))
+        ctx.enter_context(tc.manual_schedule())
+
+        raw = [keep.tile([P, J, T], F32, name="raw%d" % g, align_bytes=64) for g in range(WHOLE)]
+        grouped = [keep.tile([P, T, J], BF16, name="grouped%d" % g, align_bytes=64) for g in range(WHOLE)]
+        codes = [keep.tile([P, T], U32, name="codes%d" % g, align_bytes=64) for g in range(WHOLE)]
+        scales = [keep.tile([P, T], U8, name="scales%d" % g, align_bytes=64) for g in range(WHOLE)]
+        half_raw = {u: keep.tile([P, J, HALF], F32, name="raw%d_%d" % u, align_bytes=64) for u in HALVES}
+        half_grouped = {u: keep.tile([P, HALF, J], BF16, name="grouped%d_%d" % u, align_bytes=64) for u in HALVES}
+        half_codes = {u: keep.tile([P, HALF], U32, name="codes%d_%d" % u, align_bytes=64) for u in HALVES}
+        half_scales = {u: keep.tile([P, HALF], U8, name="scales%d_%d" % u, align_bytes=64) for u in HALVES}
+        w8 = keep.tile([P, W8_PASSES, D * 4], U8, name="w8", align_bytes=64)
+        w4 = keep.tile([P, W4_PASSES, D * 2], U8, name="w4", align_bytes=64)
+        w8_plane = keep.tile([P, W8_PASSES * D], U8, name="w8_plane", align_bytes=64)
+        w4_plane = keep.tile([P, W4_PASSES * D], U8, name="w4_plane", align_bytes=64)
+        result = [keep.tile([P, D], F32, name="result%d" % b, align_bytes=64) for b in range(BLOCKS)]
+        table_in = keep.tile([P, 1], F32, name="table_in")
+        table_out = keep.tile([P, 1], F32, name="table_out")
+        acc = [psum.tile([P, D], F32, name="acc%d" % b) for b in range(BLOCKS)]
+
+        nc.vector.memset(w8_plane[:].bitcast(I32), 0)
+        nc.vector.memset(w4_plane[:].bitcast(I32), 0)
+        nc.vector.memset(table_in[:], 0.0)
+
+        load_scales(nc, w8_plane, w8_scales, W8_PASSES)
+        nc.sync.dma_start(out=raw[0][:], in_=dy_rows[0])
+        nc.sync.dma_start(
+            out=w8[:].rearrange("p a b -> p (a b)").bitcast(I32).rearrange("p (a b) -> p a b", a=W8_PASSES),
+            in_=w8_words.rearrange("a p d i -> p a (d i)").bitcast(I32),
+        )
+        nc.sync.dma_start(out=raw[1][:], in_=dy_rows[1])
+        nc.sync.dma_start(
+            out=w4[:].rearrange("p a b -> p (a b)").bitcast(I32).rearrange("p (a b) -> p a b", a=W4_PASSES),
+            in_=w4_words.rearrange("a p b -> p a b").bitcast(I32),
+        )
+        nc.scalar.copy(out=table_out[:], in_=table_in[:])
+        load_scales(nc, w4_plane, w4_scales, W4_PASSES)
+        nc.sync.dma_start(out=raw[2][:], in_=dy_rows[2])
+        for g, h in HALVES:
+            nc.sync.dma_start(out=half_raw[g, h][:], in_=dy_rows[g][:, :, h * HALF : (h + 1) * HALF])
+
+        def multiply(g, b, b_codes, b_scales):
+            if g < W8_PASSES:
+                words = w8[:, g, :].bitcast(E4M3X4)
+                plane = w8_plane[:, g * D : (g + 1) * D]
+            else:
+                a = g - W8_PASSES
+                words = w4[:, a, :].bitcast(E2M1X4)
+                plane = w4_plane[:, a * D : (a + 1) * D]
+            nc.tensor.matmul_mx(
+                out=acc[b][:],
+                lhsT=b_codes.bitcast(E5M2X4),
+                lhsT_scale=b_scales,
+                rhs=words,
+                rhs_scale=plane,
+                start=(g == 0),
+                stop=(g == PASSES - 1),
+            )
+
+        for g in range(WHOLE):
+            interleave(nc.scalar.copy, grouped[g], raw[g], V_COLS, T)
+            interleave(nc.vector.tensor_copy, grouped[g], raw[g], 0, HALF)
+            interleave(nc.vector.tensor_copy, grouped[g], raw[g], HALF, V_COLS)
+            for t0 in (0, HALF):
+                nc.vector.quantize_mx(
+                    out=codes[g][:, t0 : t0 + HALF].bitcast(E5M2X4),
+                    scales=scales[g][:, t0 : t0 + HALF],
+                    in_=grouped[g][:, t0 : t0 + HALF, :].rearrange("p t j -> p (t j)"),
+                )
+            for b in range(BLOCKS):
+                cols = slice(b * P, (b + 1) * P)
+                multiply(g, b, codes[g][:, cols], scales[g][:, cols])
+
+        def finish(copy, b, d0, d1):
+            copy(out=result[b][:, d0:d1], in_=acc[b][:, d0:d1])
+            nc.sync.dma_start(out=out[b * P : (b + 1) * P, d0:d1], in_=result[b][:, d0:d1])
+
+        for u in HALVES:
+            g, h = u
+            interleave(nc.scalar.copy, half_grouped[u], half_raw[u], V_HALF, HALF)
+            interleave(nc.vector.tensor_copy, half_grouped[u], half_raw[u], 0, V_HALF)
+            for b in (0, 1):
+                cols = slice(b * P, (b + 1) * P)
+                nc.vector.quantize_mx(
+                    out=half_codes[u][:, cols].bitcast(E5M2X4),
+                    scales=half_scales[u][:, cols],
+                    in_=half_grouped[u][:, cols, :].rearrange("p t j -> p (t j)"),
+                )
+                multiply(g, 2 * h + b, half_codes[u][:, cols], half_scales[u][:, cols])
+            if u == (3, 1):
+                finish(nc.scalar.copy, 0, 0, D)
+        finish(nc.scalar.copy, 1, 0, D)
+        finish(nc.scalar.copy, 2, 0, D)
+        finish(nc.vector.tensor_copy, 3, 0, D // 2)
+        finish(nc.vector.tensor_copy, 3, D // 2, D)

@@ -20,17 +20,14 @@ PASSES = 5
 W8_PASSES = 2
 W4_PASSES = 3
 BLOCKS = 4
-HALF = T // 2
-V_COLS = 320
-V_HALF = 160
-WHOLE = 3
-HALVES = ((3, 0), (4, 0), (3, 1), (4, 1))
+V_COLS = 288
+LOAD_ORDER = (2, 3, 0, 4, 1)
 
 
 def load_scales(nc, plane, scales, passes):
     rows = scales.bitcast(I32).rearrange("a (q r) d -> r q a d", r=4)
     for r in range(4):
-        nc.scalar.dma_start(
+        nc.sync.dma_start(
             out=plane[r:P:32, :].bitcast(I32).rearrange("q (a d) -> q a d", a=passes), in_=rows[r]
         )
 
@@ -51,95 +48,81 @@ def tile_mix_dyq_tm_none_kernel(tc, dy, w8_words, w8_scales, w4_words, w4_scales
         psum = ctx.enter_context(tc.psum_pool(name="psum", bufs=1))
         ctx.enter_context(tc.manual_schedule())
 
-        raw = [keep.tile([P, J, T], F32, name="raw%d" % g, align_bytes=64) for g in range(WHOLE)]
-        grouped = [keep.tile([P, T, J], BF16, name="grouped%d" % g, align_bytes=64) for g in range(WHOLE)]
-        codes = [keep.tile([P, T], U32, name="codes%d" % g, align_bytes=64) for g in range(WHOLE)]
-        scales = [keep.tile([P, T], U8, name="scales%d" % g, align_bytes=64) for g in range(WHOLE)]
-        half_raw = {u: keep.tile([P, J, HALF], F32, name="raw%d_%d" % u, align_bytes=64) for u in HALVES}
-        half_grouped = {u: keep.tile([P, HALF, J], BF16, name="grouped%d_%d" % u, align_bytes=64) for u in HALVES}
-        half_codes = {u: keep.tile([P, HALF], U32, name="codes%d_%d" % u, align_bytes=64) for u in HALVES}
-        half_scales = {u: keep.tile([P, HALF], U8, name="scales%d_%d" % u, align_bytes=64) for u in HALVES}
-        w8 = keep.tile([P, W8_PASSES, D * 4], U8, name="w8", align_bytes=64)
+        raw = [keep.tile([P, J, T], F32, name="raw%d" % g, align_bytes=64) for g in range(PASSES)]
+        grouped = [keep.tile([P, T, J], BF16, name="grouped%d" % g, align_bytes=64) for g in range(PASSES)]
+        codes = [keep.tile([P, T], U32, name="codes%d" % g, align_bytes=64) for g in range(PASSES)]
+        scales = [keep.tile([P, T], U8, name="scales%d" % g, align_bytes=64) for g in range(PASSES)]
+        w8 = [keep.tile([P, D * 4], U8, name="w8_%d" % g, align_bytes=64) for g in range(W8_PASSES)]
         w4 = keep.tile([P, W4_PASSES, D * 2], U8, name="w4", align_bytes=64)
         w8_plane = keep.tile([P, W8_PASSES * D], U8, name="w8_plane", align_bytes=64)
         w4_plane = keep.tile([P, W4_PASSES * D], U8, name="w4_plane", align_bytes=64)
         result = [keep.tile([P, D], F32, name="result%d" % b, align_bytes=64) for b in range(BLOCKS)]
-        table_in = keep.tile([P, 1], F32, name="table_in")
-        table_out = keep.tile([P, 1], F32, name="table_out")
         acc = [psum.tile([P, D], F32, name="acc%d" % b) for b in range(BLOCKS)]
 
-        nc.vector.memset(w8_plane[:].bitcast(I32), 0)
         nc.vector.memset(w4_plane[:].bitcast(I32), 0)
-        nc.vector.memset(table_in[:], 0.0)
+        nc.vector.memset(w8_plane[:].bitcast(I32), 0)
 
-        load_scales(nc, w8_plane, w8_scales, W8_PASSES)
-        nc.sync.dma_start(out=raw[0][:], in_=dy_rows[0])
-        nc.sync.dma_start(
-            out=w8[:].rearrange("p a b -> p (a b)").bitcast(I32).rearrange("p (a b) -> p a b", a=W8_PASSES),
-            in_=w8_words.rearrange("a p d i -> p a (d i)").bitcast(I32),
-        )
-        nc.sync.dma_start(out=raw[1][:], in_=dy_rows[1])
+        def load_dy(g):
+            nc.sync.dma_start(out=raw[g][:], in_=dy_rows[g])
+
+        load_dy(2)
+        load_dy(3)
+        load_scales(nc, w4_plane, w4_scales, W4_PASSES)
+        load_dy(0)
         nc.sync.dma_start(
             out=w4[:].rearrange("p a b -> p (a b)").bitcast(I32).rearrange("p (a b) -> p a b", a=W4_PASSES),
             in_=w4_words.rearrange("a p b -> p a b").bitcast(I32),
         )
-        nc.scalar.copy(out=table_out[:], in_=table_in[:])
-        load_scales(nc, w4_plane, w4_scales, W4_PASSES)
-        nc.sync.dma_start(out=raw[2][:], in_=dy_rows[2])
-        for g, h in HALVES:
-            nc.sync.dma_start(out=half_raw[g, h][:], in_=dy_rows[g][:, :, h * HALF : (h + 1) * HALF])
+        load_scales(nc, w8_plane, w8_scales, W8_PASSES)
+        load_dy(4)
+        load_dy(1)
+        for g in range(W8_PASSES):
+            nc.sync.dma_start(
+                out=w8[g][:].bitcast(I32), in_=w8_words[g].rearrange("p d i -> p (d i)").bitcast(I32)
+            )
 
-        def multiply(g, b, b_codes, b_scales):
+        for g in LOAD_ORDER:
+            interleave(nc.scalar.copy, grouped[g], raw[g], V_COLS, T)
+            interleave(nc.vector.tensor_copy, grouped[g], raw[g], 0, P)
+            interleave(nc.vector.tensor_copy, grouped[g], raw[g], P, V_COLS)
+            for t0, t1 in ((0, P), (P, 2 * P), (2 * P, T)):
+                nc.vector.quantize_mx(
+                    out=codes[g][:, t0:t1].bitcast(E5M2X4),
+                    scales=scales[g][:, t0:t1],
+                    in_=grouped[g][:, t0:t1, :].rearrange("p t j -> p (t j)"),
+                )
+
+        def multiply(g, b):
             if g < W8_PASSES:
-                words = w8[:, g, :].bitcast(E4M3X4)
+                words = w8[g][:].bitcast(E4M3X4)
                 plane = w8_plane[:, g * D : (g + 1) * D]
             else:
                 a = g - W8_PASSES
                 words = w4[:, a, :].bitcast(E2M1X4)
                 plane = w4_plane[:, a * D : (a + 1) * D]
+            cols = slice(b * P, (b + 1) * P)
             nc.tensor.matmul_mx(
                 out=acc[b][:],
-                lhsT=b_codes.bitcast(E5M2X4),
-                lhsT_scale=b_scales,
+                lhsT=codes[g][:, cols].bitcast(E5M2X4),
+                lhsT_scale=scales[g][:, cols],
                 rhs=words,
                 rhs_scale=plane,
-                start=(g == 0),
-                stop=(g == PASSES - 1),
+                start=(g == W8_PASSES),
+                stop=(g == W8_PASSES - 1),
             )
 
-        for g in range(WHOLE):
-            interleave(nc.scalar.copy, grouped[g], raw[g], V_COLS, T)
-            interleave(nc.vector.tensor_copy, grouped[g], raw[g], 0, HALF)
-            interleave(nc.vector.tensor_copy, grouped[g], raw[g], HALF, V_COLS)
-            for t0 in (0, HALF):
-                nc.vector.quantize_mx(
-                    out=codes[g][:, t0 : t0 + HALF].bitcast(E5M2X4),
-                    scales=scales[g][:, t0 : t0 + HALF],
-                    in_=grouped[g][:, t0 : t0 + HALF, :].rearrange("p t j -> p (t j)"),
-                )
+        for g in range(W8_PASSES, PASSES):
             for b in range(BLOCKS):
-                cols = slice(b * P, (b + 1) * P)
-                multiply(g, b, codes[g][:, cols], scales[g][:, cols])
+                multiply(g, b)
+        for g, b in ((0, 0), (0, 1), (1, 0), (1, 1), (0, 2), (1, 2), (0, 3), (1, 3)):
+            multiply(g, b)
 
         def finish(copy, b, d0, d1):
             copy(out=result[b][:, d0:d1], in_=acc[b][:, d0:d1])
             nc.sync.dma_start(out=out[b * P : (b + 1) * P, d0:d1], in_=result[b][:, d0:d1])
 
-        for u in HALVES:
-            g, h = u
-            interleave(nc.scalar.copy, half_grouped[u], half_raw[u], V_HALF, HALF)
-            interleave(nc.vector.tensor_copy, half_grouped[u], half_raw[u], 0, V_HALF)
-            for b in (0, 1):
-                cols = slice(b * P, (b + 1) * P)
-                nc.vector.quantize_mx(
-                    out=half_codes[u][:, cols].bitcast(E5M2X4),
-                    scales=half_scales[u][:, cols],
-                    in_=half_grouped[u][:, cols, :].rearrange("p t j -> p (t j)"),
-                )
-                multiply(g, 2 * h + b, half_codes[u][:, cols], half_scales[u][:, cols])
-            if u == (3, 1):
-                finish(nc.scalar.copy, 0, 0, D)
-        finish(nc.scalar.copy, 1, 0, D)
+        finish(nc.scalar.copy, 0, 0, D // 2)
+        finish(nc.scalar.copy, 0, D // 2, D)
+        finish(nc.vector.tensor_copy, 1, 0, D)
         finish(nc.scalar.copy, 2, 0, D)
-        finish(nc.vector.tensor_copy, 3, 0, D // 2)
-        finish(nc.vector.tensor_copy, 3, D // 2, D)
+        finish(nc.vector.tensor_copy, 3, 0, D)

@@ -21,7 +21,9 @@ W8_PASSES = 2
 W4_PASSES = 3
 BLOCKS = 4
 V_COLS = 288
-LOAD_ORDER = (2, 3, 0, 4, 1)
+WHOLE = (2, 3, 4, 0)
+LAST = 1
+V_EARLY = 144
 
 
 def load_scales(nc, plane, scales, passes):
@@ -32,10 +34,10 @@ def load_scales(nc, plane, scales, passes):
         )
 
 
-def interleave(copy, grouped, raw, t0, t1):
+def interleave(copy, grouped, raw, t0, t1, base=0):
     copy(
         out=grouped[:, t0:t1, :].rearrange("p (c i) j -> p c j i", i=4),
-        in_=raw[:, :, t0:t1].rearrange("p j (c i) -> p c j i", i=4),
+        in_=raw[:, :, t0 - base : t1 - base].rearrange("p j (c i) -> p c j i", i=4),
     )
 
 
@@ -48,7 +50,9 @@ def tile_mix_dyq_tm_none_kernel(tc, dy, w8_words, w8_scales, w4_words, w4_scales
         psum = ctx.enter_context(tc.psum_pool(name="psum", bufs=1))
         ctx.enter_context(tc.manual_schedule())
 
-        raw = [keep.tile([P, J, T], F32, name="raw%d" % g, align_bytes=64) for g in range(PASSES)]
+        raw = {g: keep.tile([P, J, T], F32, name="raw%d" % g, align_bytes=64) for g in WHOLE}
+        early_raw = keep.tile([P, J, 2 * P], F32, name="early_raw", align_bytes=64)
+        late_raw = {b: keep.tile([P, J, P], F32, name="late_raw%d" % b, align_bytes=64) for b in (2, 3)}
         grouped = [keep.tile([P, T, J], BF16, name="grouped%d" % g, align_bytes=64) for g in range(PASSES)]
         codes = [keep.tile([P, T], U32, name="codes%d" % g, align_bytes=64) for g in range(PASSES)]
         scales = [keep.tile([P, T], U8, name="scales%d" % g, align_bytes=64) for g in range(PASSES)]
@@ -68,31 +72,29 @@ def tile_mix_dyq_tm_none_kernel(tc, dy, w8_words, w8_scales, w4_words, w4_scales
         load_dy(2)
         load_dy(3)
         load_scales(nc, w4_plane, w4_scales, W4_PASSES)
-        load_dy(0)
         nc.sync.dma_start(
             out=w4[:].rearrange("p a b -> p (a b)").bitcast(I32).rearrange("p (a b) -> p a b", a=W4_PASSES),
             in_=w4_words.rearrange("a p b -> p a b").bitcast(I32),
         )
-        load_scales(nc, w8_plane, w8_scales, W8_PASSES)
         load_dy(4)
-        load_dy(1)
-        for g in range(W8_PASSES):
+        load_scales(nc, w8_plane, w8_scales, W8_PASSES)
+        nc.sync.dma_start(out=early_raw[:], in_=dy_rows[LAST][:, :, 0 : 2 * P])
+        load_dy(0)
+        for g in (1, 0):
             nc.sync.dma_start(
                 out=w8[g][:].bitcast(I32), in_=w8_words[g].rearrange("p d i -> p (d i)").bitcast(I32)
             )
+        for b in (2, 3):
+            nc.sync.dma_start(out=late_raw[b][:], in_=dy_rows[LAST][:, :, b * P : (b + 1) * P])
 
-        for g in LOAD_ORDER:
-            interleave(nc.scalar.copy, grouped[g], raw[g], V_COLS, T)
-            interleave(nc.vector.tensor_copy, grouped[g], raw[g], 0, P)
-            interleave(nc.vector.tensor_copy, grouped[g], raw[g], P, V_COLS)
-            for t0, t1 in ((0, P), (P, 2 * P), (2 * P, T)):
-                nc.vector.quantize_mx(
-                    out=codes[g][:, t0:t1].bitcast(E5M2X4),
-                    scales=scales[g][:, t0:t1],
-                    in_=grouped[g][:, t0:t1, :].rearrange("p t j -> p (t j)"),
-                )
+        def quantise(g, t0, t1):
+            nc.vector.quantize_mx(
+                out=codes[g][:, t0:t1].bitcast(E5M2X4),
+                scales=scales[g][:, t0:t1],
+                in_=grouped[g][:, t0:t1, :].rearrange("p t j -> p (t j)"),
+            )
 
-        def multiply(g, b):
+        def multiply(g, b, stop=False):
             if g < W8_PASSES:
                 words = w8[g][:].bitcast(E4M3X4)
                 plane = w8_plane[:, g * D : (g + 1) * D]
@@ -108,21 +110,52 @@ def tile_mix_dyq_tm_none_kernel(tc, dy, w8_words, w8_scales, w4_words, w4_scales
                 rhs=words,
                 rhs_scale=plane,
                 start=(g == W8_PASSES),
-                stop=(g == W8_PASSES - 1),
+                stop=stop,
             )
-
-        for g in range(W8_PASSES, PASSES):
-            for b in range(BLOCKS):
-                multiply(g, b)
-        for g, b in ((0, 0), (0, 1), (1, 0), (1, 1), (0, 2), (1, 2), (0, 3), (1, 3)):
-            multiply(g, b)
 
         def finish(copy, b, d0, d1):
             copy(out=result[b][:, d0:d1], in_=acc[b][:, d0:d1])
             nc.sync.dma_start(out=out[b * P : (b + 1) * P, d0:d1], in_=result[b][:, d0:d1])
 
+        def late(b):
+            halves = ((b * P, b * P + P // 2), (b * P + P // 2, (b + 1) * P))
+            for t0, t1 in halves:
+                interleave(nc.vector.tensor_copy, grouped[LAST], late_raw[b], t0, t1, b * P)
+            for t0, t1 in halves:
+                quantise(LAST, t0, t1)
+
+        def whole(g):
+            interleave(nc.scalar.copy, grouped[g], raw[g], V_COLS, T)
+            interleave(nc.vector.tensor_copy, grouped[g], raw[g], 0, P)
+            interleave(nc.vector.tensor_copy, grouped[g], raw[g], P, V_COLS)
+            quantise(g, 0, P)
+            quantise(g, P, 2 * P)
+            quantise(g, 2 * P, T)
+
+        for g in range(W8_PASSES, PASSES):
+            whole(g)
+            for b in range(BLOCKS):
+                multiply(g, b)
+        interleave(nc.scalar.copy, grouped[LAST], early_raw, V_EARLY, 2 * P)
+        interleave(nc.vector.tensor_copy, grouped[LAST], early_raw, 0, P)
+        interleave(nc.vector.tensor_copy, grouped[LAST], early_raw, P, V_EARLY)
+        quantise(LAST, 0, P)
+        quantise(LAST, P, 2 * P)
+        whole(0)
+        multiply(1, 0)
+        multiply(1, 1)
+        multiply(0, 0, stop=True)
+        multiply(0, 1, stop=True)
+        multiply(0, 2)
+        multiply(0, 3)
         finish(nc.scalar.copy, 0, 0, D // 2)
         finish(nc.scalar.copy, 0, D // 2, D)
-        finish(nc.vector.tensor_copy, 1, 0, D)
-        finish(nc.scalar.copy, 2, 0, D)
-        finish(nc.vector.tensor_copy, 3, 0, D)
+        finish(nc.scalar.copy, 1, 0, D)
+        late(2)
+        multiply(LAST, 2, stop=True)
+        late(3)
+        multiply(LAST, 3, stop=True)
+        finish(nc.scalar.copy, 2, 0, D // 2)
+        finish(nc.scalar.copy, 2, D // 2, D)
+        finish(nc.vector.tensor_copy, 3, 0, D // 2)
+        finish(nc.vector.tensor_copy, 3, D // 2, D)

@@ -23,7 +23,8 @@ BLOCKS = 4
 V_COLS = 288
 WHOLE = (2, 3, 4, 0)
 LAST = 1
-V_EARLY = 144
+EARLY = T - P
+V_EARLY = 208
 
 
 def load_scales(nc, plane, scales, passes):
@@ -51,8 +52,8 @@ def tile_mix_dyq_tm_none_kernel(tc, dy, w8_words, w8_scales, w4_words, w4_scales
         ctx.enter_context(tc.manual_schedule())
 
         raw = {g: keep.tile([P, J, T], F32, name="raw%d" % g, align_bytes=64) for g in WHOLE}
-        early_raw = keep.tile([P, J, 2 * P], F32, name="early_raw", align_bytes=64)
-        late_raw = {b: keep.tile([P, J, P], F32, name="late_raw%d" % b, align_bytes=64) for b in (2, 3)}
+        early_raw = keep.tile([P, J, EARLY], F32, name="early_raw", align_bytes=64)
+        late_raw = keep.tile([P, J, P], F32, name="late_raw", align_bytes=64)
         grouped = [keep.tile([P, T, J], BF16, name="grouped%d" % g, align_bytes=64) for g in range(PASSES)]
         codes = [keep.tile([P, T], U32, name="codes%d" % g, align_bytes=64) for g in range(PASSES)]
         scales = [keep.tile([P, T], U8, name="scales%d" % g, align_bytes=64) for g in range(PASSES)]
@@ -72,20 +73,19 @@ def tile_mix_dyq_tm_none_kernel(tc, dy, w8_words, w8_scales, w4_words, w4_scales
         load_dy(2)
         load_dy(3)
         load_scales(nc, w4_plane, w4_scales, W4_PASSES)
+        nc.sync.dma_start(out=early_raw[:], in_=dy_rows[LAST][:, :, 0:EARLY])
         nc.sync.dma_start(
             out=w4[:].rearrange("p a b -> p (a b)").bitcast(I32).rearrange("p (a b) -> p a b", a=W4_PASSES),
             in_=w4_words.rearrange("a p b -> p a b").bitcast(I32),
         )
-        load_dy(4)
         load_scales(nc, w8_plane, w8_scales, W8_PASSES)
-        nc.sync.dma_start(out=early_raw[:], in_=dy_rows[LAST][:, :, 0 : 2 * P])
+        load_dy(4)
         load_dy(0)
         for g in (1, 0):
             nc.sync.dma_start(
                 out=w8[g][:].bitcast(I32), in_=w8_words[g].rearrange("p d i -> p (d i)").bitcast(I32)
             )
-        for b in (2, 3):
-            nc.sync.dma_start(out=late_raw[b][:], in_=dy_rows[LAST][:, :, b * P : (b + 1) * P])
+        nc.sync.dma_start(out=late_raw[:], in_=dy_rows[LAST][:, :, EARLY:T])
 
         def quantise(g, t0, t1):
             nc.vector.quantize_mx(
@@ -117,13 +117,6 @@ def tile_mix_dyq_tm_none_kernel(tc, dy, w8_words, w8_scales, w4_words, w4_scales
             copy(out=result[b][:, d0:d1], in_=acc[b][:, d0:d1])
             nc.sync.dma_start(out=out[b * P : (b + 1) * P, d0:d1], in_=result[b][:, d0:d1])
 
-        def late(b):
-            halves = ((b * P, b * P + P // 2), (b * P + P // 2, (b + 1) * P))
-            for t0, t1 in halves:
-                interleave(nc.vector.tensor_copy, grouped[LAST], late_raw[b], t0, t1, b * P)
-            for t0, t1 in halves:
-                quantise(LAST, t0, t1)
-
         def whole(g):
             interleave(nc.scalar.copy, grouped[g], raw[g], V_COLS, T)
             interleave(nc.vector.tensor_copy, grouped[g], raw[g], 0, P)
@@ -132,30 +125,34 @@ def tile_mix_dyq_tm_none_kernel(tc, dy, w8_words, w8_scales, w4_words, w4_scales
             quantise(g, P, 2 * P)
             quantise(g, 2 * P, T)
 
-        for g in range(W8_PASSES, PASSES):
-            whole(g)
-            for b in range(BLOCKS):
-                multiply(g, b)
-        interleave(nc.scalar.copy, grouped[LAST], early_raw, V_EARLY, 2 * P)
+        whole(2)
+        whole(3)
+        interleave(nc.scalar.copy, grouped[LAST], early_raw, V_EARLY, EARLY)
         interleave(nc.vector.tensor_copy, grouped[LAST], early_raw, 0, P)
         interleave(nc.vector.tensor_copy, grouped[LAST], early_raw, P, V_EARLY)
         quantise(LAST, 0, P)
-        quantise(LAST, P, 2 * P)
+        quantise(LAST, P, EARLY)
+        whole(4)
         whole(0)
+        for g in range(W8_PASSES, PASSES):
+            for b in range(BLOCKS):
+                multiply(g, b)
         multiply(1, 0)
         multiply(1, 1)
         multiply(0, 0, stop=True)
         multiply(0, 1, stop=True)
-        multiply(0, 2)
+        multiply(1, 2)
+        multiply(0, 2, stop=True)
         multiply(0, 3)
         finish(nc.scalar.copy, 0, 0, D // 2)
         finish(nc.scalar.copy, 0, D // 2, D)
         finish(nc.scalar.copy, 1, 0, D)
-        late(2)
-        multiply(LAST, 2, stop=True)
-        late(3)
+
+        halves = ((EARLY, EARLY + P // 2), (EARLY + P // 2, T))
+        for t0, t1 in halves:
+            interleave(nc.vector.tensor_copy, grouped[LAST], late_raw, t0, t1, EARLY)
+        for t0, t1 in halves:
+            quantise(LAST, t0, t1)
         multiply(LAST, 3, stop=True)
-        finish(nc.scalar.copy, 2, 0, D // 2)
-        finish(nc.scalar.copy, 2, D // 2, D)
-        finish(nc.vector.tensor_copy, 3, 0, D // 2)
-        finish(nc.vector.tensor_copy, 3, D // 2, D)
+        finish(nc.vector.tensor_copy, 2, 0, D)
+        finish(nc.vector.tensor_copy, 3, 0, D)

@@ -19,11 +19,10 @@ J = 4
 PASSES = 5
 W8_PASSES = 2
 W4_PASSES = 3
-BLOCKS = 4
-V_COLS = 288
-WHOLE = (2, 3, 4, 0)
-LAST = 1
+TILES = 4
+SPLIT = 1
 EARLY = T - P
+V_WHOLE = 288
 V_EARLY = 208
 
 
@@ -51,7 +50,10 @@ def tile_mix_dyq_tm_none_kernel(tc, dy, w8_words, w8_scales, w4_words, w4_scales
         psum = ctx.enter_context(tc.psum_pool(name="psum", bufs=1))
         ctx.enter_context(tc.manual_schedule())
 
-        raw = {g: keep.tile([P, J, T], F32, name="raw%d" % g, align_bytes=64) for g in WHOLE}
+        first_raw = keep.tile([P, 2, J, T], F32, name="first_raw", align_bytes=64)
+        raw = {g: keep.tile([P, J, T], F32, name="raw%d" % g, align_bytes=64) for g in (4, 0)}
+        raw[2] = first_raw[:, 0, :, :]
+        raw[3] = first_raw[:, 1, :, :]
         early_raw = keep.tile([P, J, EARLY], F32, name="early_raw", align_bytes=64)
         late_raw = keep.tile([P, J, P], F32, name="late_raw", align_bytes=64)
         grouped = [keep.tile([P, T, J], BF16, name="grouped%d" % g, align_bytes=64) for g in range(PASSES)]
@@ -61,31 +63,33 @@ def tile_mix_dyq_tm_none_kernel(tc, dy, w8_words, w8_scales, w4_words, w4_scales
         w4 = keep.tile([P, W4_PASSES, D * 2], U8, name="w4", align_bytes=64)
         w8_plane = keep.tile([P, W8_PASSES * D], U8, name="w8_plane", align_bytes=64)
         w4_plane = keep.tile([P, W4_PASSES * D], U8, name="w4_plane", align_bytes=64)
-        result = [keep.tile([P, D], F32, name="result%d" % b, align_bytes=64) for b in range(BLOCKS)]
-        acc = [psum.tile([P, D], F32, name="acc%d" % b) for b in range(BLOCKS)]
+        result = [keep.tile([P, D], F32, name="result%d" % b, align_bytes=64) for b in range(TILES)]
+        acc = [psum.tile([P, D], F32, name="acc%d" % b) for b in range(TILES)]
 
         nc.vector.memset(w4_plane[:].bitcast(I32), 0)
         nc.vector.memset(w8_plane[:].bitcast(I32), 0)
 
-        def load_dy(g):
+        def load_whole(g):
             nc.sync.dma_start(out=raw[g][:], in_=dy_rows[g])
 
-        load_dy(2)
-        load_dy(3)
+        nc.sync.dma_start(
+            out=first_raw[:].rearrange("p g j t -> p g (j t)"),
+            in_=dy_rows[2:4].rearrange("g p j t -> p g (j t)"),
+        )
         load_scales(nc, w4_plane, w4_scales, W4_PASSES)
-        nc.sync.dma_start(out=early_raw[:], in_=dy_rows[LAST][:, :, 0:EARLY])
+        nc.sync.dma_start(out=early_raw[:], in_=dy_rows[SPLIT][:, :, 0:EARLY])
         nc.sync.dma_start(
             out=w4[:].rearrange("p a b -> p (a b)").bitcast(I32).rearrange("p (a b) -> p a b", a=W4_PASSES),
             in_=w4_words.rearrange("a p b -> p a b").bitcast(I32),
         )
         load_scales(nc, w8_plane, w8_scales, W8_PASSES)
-        load_dy(4)
-        load_dy(0)
+        load_whole(4)
+        load_whole(0)
         for g in (1, 0):
             nc.sync.dma_start(
                 out=w8[g][:].bitcast(I32), in_=w8_words[g].rearrange("p d i -> p (d i)").bitcast(I32)
             )
-        nc.sync.dma_start(out=late_raw[:], in_=dy_rows[LAST][:, :, EARLY:T])
+        nc.sync.dma_start(out=late_raw[:], in_=dy_rows[SPLIT][:, :, EARLY:T])
 
         def quantise(g, t0, t1):
             nc.vector.quantize_mx(
@@ -93,6 +97,15 @@ def tile_mix_dyq_tm_none_kernel(tc, dy, w8_words, w8_scales, w4_words, w4_scales
                 scales=scales[g][:, t0:t1],
                 in_=grouped[g][:, t0:t1, :].rearrange("p t j -> p (t j)"),
             )
+
+        def prepare_whole(g):
+            interleave(nc.scalar.copy, grouped[g], raw[g], V_WHOLE, T)
+            interleave(nc.vector.tensor_copy, grouped[g], raw[g], 0, P)
+            interleave(nc.vector.tensor_copy, grouped[g], raw[g], P, 2 * P)
+            quantise(g, 0, P)
+            interleave(nc.vector.tensor_copy, grouped[g], raw[g], 2 * P, V_WHOLE)
+            quantise(g, P, 2 * P)
+            quantise(g, 2 * P, T)
 
         def multiply(g, b, stop=False):
             if g < W8_PASSES:
@@ -117,25 +130,18 @@ def tile_mix_dyq_tm_none_kernel(tc, dy, w8_words, w8_scales, w4_words, w4_scales
             copy(out=result[b][:, d0:d1], in_=acc[b][:, d0:d1])
             nc.sync.dma_start(out=out[b * P : (b + 1) * P, d0:d1], in_=result[b][:, d0:d1])
 
-        def whole(g):
-            interleave(nc.scalar.copy, grouped[g], raw[g], V_COLS, T)
-            interleave(nc.vector.tensor_copy, grouped[g], raw[g], 0, P)
-            interleave(nc.vector.tensor_copy, grouped[g], raw[g], P, V_COLS)
-            quantise(g, 0, P)
-            quantise(g, P, 2 * P)
-            quantise(g, 2 * P, T)
+        prepare_whole(2)
+        prepare_whole(3)
+        interleave(nc.scalar.copy, grouped[SPLIT], early_raw, V_EARLY, EARLY)
+        interleave(nc.vector.tensor_copy, grouped[SPLIT], early_raw, 0, P)
+        interleave(nc.vector.tensor_copy, grouped[SPLIT], early_raw, P, V_EARLY)
+        quantise(SPLIT, 0, P)
+        quantise(SPLIT, P, EARLY)
+        prepare_whole(4)
+        prepare_whole(0)
 
-        whole(2)
-        whole(3)
-        interleave(nc.scalar.copy, grouped[LAST], early_raw, V_EARLY, EARLY)
-        interleave(nc.vector.tensor_copy, grouped[LAST], early_raw, 0, P)
-        interleave(nc.vector.tensor_copy, grouped[LAST], early_raw, P, V_EARLY)
-        quantise(LAST, 0, P)
-        quantise(LAST, P, EARLY)
-        whole(4)
-        whole(0)
         for g in range(W8_PASSES, PASSES):
-            for b in range(BLOCKS):
+            for b in range(TILES):
                 multiply(g, b)
         multiply(1, 0)
         multiply(1, 1)
@@ -144,15 +150,16 @@ def tile_mix_dyq_tm_none_kernel(tc, dy, w8_words, w8_scales, w4_words, w4_scales
         multiply(1, 2)
         multiply(0, 2, stop=True)
         multiply(0, 3)
+
         finish(nc.scalar.copy, 0, 0, D // 2)
         finish(nc.scalar.copy, 0, D // 2, D)
         finish(nc.scalar.copy, 1, 0, D)
 
         halves = ((EARLY, EARLY + P // 2), (EARLY + P // 2, T))
         for t0, t1 in halves:
-            interleave(nc.vector.tensor_copy, grouped[LAST], late_raw, t0, t1, EARLY)
+            interleave(nc.vector.tensor_copy, grouped[SPLIT], late_raw, t0, t1, EARLY)
         for t0, t1 in halves:
-            quantise(LAST, t0, t1)
-        multiply(LAST, 3, stop=True)
+            quantise(SPLIT, t0, t1)
+        multiply(SPLIT, 3, stop=True)
         finish(nc.vector.tensor_copy, 2, 0, D)
         finish(nc.vector.tensor_copy, 3, 0, D)

@@ -22,6 +22,8 @@ W4_PASSES = 3
 TILES = 4
 SPLIT = 1
 EARLY = T - P
+H = D // 2
+HALVED = (0, TILES - 1)
 V_WHOLE = 288
 V_EARLY = 208
 
@@ -64,7 +66,10 @@ def tile_mix_dyq_tm_none_kernel(tc, dy, w8_words, w8_scales, w4_words, w4_scales
         w8_plane = keep.tile([P, W8_PASSES * D], U8, name="w8_plane", align_bytes=64)
         w4_plane = keep.tile([P, W4_PASSES * D], U8, name="w4_plane", align_bytes=64)
         result = [keep.tile([P, D], F32, name="result%d" % b, align_bytes=64) for b in range(TILES)]
-        acc = [psum.tile([P, D], F32, name="acc%d" % b) for b in range(TILES)]
+        acc = [
+            [(d0, d1, psum.tile([P, d1 - d0], F32, name="acc%d_%d" % (b, d0))) for d0, d1 in spans]
+            for b, spans in enumerate(((0, H), (H, D)) if b in HALVED else ((0, D),) for b in range(TILES))
+        ]
 
         nc.vector.memset(w4_plane[:].bitcast(I32), 0)
         nc.vector.memset(w8_plane[:].bitcast(I32), 0)
@@ -108,27 +113,29 @@ def tile_mix_dyq_tm_none_kernel(tc, dy, w8_words, w8_scales, w4_words, w4_scales
             quantise(g, 2 * P, T)
 
         def multiply(g, b, stop=False):
-            if g < W8_PASSES:
-                words = w8[g][:].bitcast(E4M3X4)
-                plane = w8_plane[:, g * D : (g + 1) * D]
-            else:
-                a = g - W8_PASSES
-                words = w4[:, a, :].bitcast(E2M1X4)
-                plane = w4_plane[:, a * D : (a + 1) * D]
             cols = slice(b * P, (b + 1) * P)
-            nc.tensor.matmul_mx(
-                out=acc[b][:],
-                lhsT=codes[g][:, cols].bitcast(E5M2X4),
-                lhsT_scale=scales[g][:, cols],
-                rhs=words,
-                rhs_scale=plane,
-                start=(g == W8_PASSES),
-                stop=stop,
-            )
+            for d0, d1, bank in acc[b]:
+                if g < W8_PASSES:
+                    words = w8[g][:, 4 * d0 : 4 * d1].bitcast(E4M3X4)
+                    plane = w8_plane[:, g * D + d0 : g * D + d1]
+                else:
+                    a = g - W8_PASSES
+                    words = w4[:, a, 2 * d0 : 2 * d1].bitcast(E2M1X4)
+                    plane = w4_plane[:, a * D + d0 : a * D + d1]
+                nc.tensor.matmul_mx(
+                    out=bank[:],
+                    lhsT=codes[g][:, cols].bitcast(E5M2X4),
+                    lhsT_scale=scales[g][:, cols],
+                    rhs=words,
+                    rhs_scale=plane,
+                    start=(g == W8_PASSES),
+                    stop=stop,
+                )
 
-        def finish(copy, b, d0, d1):
-            copy(out=result[b][:, d0:d1], in_=acc[b][:, d0:d1])
-            nc.sync.dma_start(out=out[b * P : (b + 1) * P, d0:d1], in_=result[b][:, d0:d1])
+        def finish(b, *copies):
+            for copy, (d0, d1, bank) in zip(copies, acc[b]):
+                copy(out=result[b][:, d0:d1], in_=bank[:])
+            nc.sync.dma_start(out=out[b * P : (b + 1) * P, :], in_=result[b][:])
 
         prepare_whole(2)
         prepare_whole(3)
@@ -151,9 +158,9 @@ def tile_mix_dyq_tm_none_kernel(tc, dy, w8_words, w8_scales, w4_words, w4_scales
         multiply(0, 2, stop=True)
         multiply(0, 3)
 
-        finish(nc.scalar.copy, 0, 0, D // 2)
-        finish(nc.scalar.copy, 0, D // 2, D)
-        finish(nc.scalar.copy, 1, 0, D)
+        finish(0, nc.vector.tensor_copy, nc.scalar.copy)
+        finish(1, nc.scalar.copy)
+        finish(2, nc.scalar.copy)
 
         halves = ((EARLY, EARLY + P // 2), (EARLY + P // 2, T))
         for t0, t1 in halves:
@@ -161,5 +168,4 @@ def tile_mix_dyq_tm_none_kernel(tc, dy, w8_words, w8_scales, w4_words, w4_scales
         for t0, t1 in halves:
             quantise(SPLIT, t0, t1)
         multiply(SPLIT, 3, stop=True)
-        finish(nc.vector.tensor_copy, 2, 0, D)
-        finish(nc.vector.tensor_copy, 3, 0, D)
+        finish(3, nc.vector.tensor_copy, nc.scalar.copy)

@@ -24,7 +24,6 @@ SPLIT = 1
 EARLY = T - P
 H = D // 2
 HALVED = (0, TILES - 1)
-V_WHOLE = 288
 V_EARLY = 208
 
 
@@ -104,13 +103,11 @@ def tile_mix_dyq_tm_none_kernel(tc, dy, w8_words, w8_scales, w4_words, w4_scales
             )
 
         def prepare_whole(g):
-            interleave(nc.scalar.copy, grouped[g], raw[g], V_WHOLE, T)
-            interleave(nc.vector.tensor_copy, grouped[g], raw[g], 0, P)
-            interleave(nc.vector.tensor_copy, grouped[g], raw[g], P, 2 * P)
-            quantise(g, 0, P)
-            interleave(nc.vector.tensor_copy, grouped[g], raw[g], 2 * P, V_WHOLE)
-            quantise(g, P, 2 * P)
-            quantise(g, 2 * P, T)
+            for b in range(TILES):
+                copy = nc.vector.tensor_copy if b < TILES // 2 else nc.scalar.copy
+                interleave(copy, grouped[g], raw[g], b * P, (b + 1) * P)
+            for b in range(TILES):
+                quantise(g, b * P, (b + 1) * P)
 
         def multiply(g, b, stop=False):
             cols = slice(b * P, (b + 1) * P)

@@ -22,17 +22,18 @@ W4_PASSES = 3
 TILES = 4
 SPLIT = 1
 EARLY = T - P
-H = D // 2
-HALVED = (0, TILES - 1)
+CUTS = ((0, D // 2, 3 * D // 4, D), (0, D), (0, D // 2, D), (0, D // 2, D))
 V_EARLY = 208
 
 
-def load_scales(nc, plane, scales, passes):
-    rows = scales.bitcast(I32).rearrange("a (q r) d -> r q a d", r=4)
-    for r in range(4):
-        nc.sync.dma_start(
-            out=plane[r:P:32, :].bitcast(I32).rearrange("q (a d) -> q a d", a=passes), in_=rows[r]
-        )
+def land_scales(nc, plane, scales, g0, g1):
+    words = plane[:].bitcast(I32).rearrange("p (a d) -> p a d", a=PASSES)
+    nc.sync.dma_start(out=words[0:P:8, g0:g1, :], in_=scales.bitcast(I32).rearrange("a q d -> q a d"))
+
+
+def move_scales(nc, plane):
+    for r in range(1, 4):
+        nc.sync.dma_start(out=plane[r:P:32, :].bitcast(I32), in_=plane[8 * r : P : 32, :].bitcast(I32))
 
 
 def interleave(copy, grouped, raw, t0, t1, base=0):
@@ -51,10 +52,7 @@ def tile_mix_dyq_tm_none_kernel(tc, dy, w8_words, w8_scales, w4_words, w4_scales
         psum = ctx.enter_context(tc.psum_pool(name="psum", bufs=1))
         ctx.enter_context(tc.manual_schedule())
 
-        first_raw = keep.tile([P, 2, J, T], F32, name="first_raw", align_bytes=64)
-        raw = {g: keep.tile([P, J, T], F32, name="raw%d" % g, align_bytes=64) for g in (4, 0)}
-        raw[2] = first_raw[:, 0, :, :]
-        raw[3] = first_raw[:, 1, :, :]
+        raw = {g: keep.tile([P, J, T], F32, name="raw%d" % g, align_bytes=64) for g in range(PASSES) if g != SPLIT}
         early_raw = keep.tile([P, J, EARLY], F32, name="early_raw", align_bytes=64)
         late_raw = keep.tile([P, J, P], F32, name="late_raw", align_bytes=64)
         grouped = [keep.tile([P, T, J], BF16, name="grouped%d" % g, align_bytes=64) for g in range(PASSES)]
@@ -62,33 +60,29 @@ def tile_mix_dyq_tm_none_kernel(tc, dy, w8_words, w8_scales, w4_words, w4_scales
         scales = [keep.tile([P, T], U8, name="scales%d" % g, align_bytes=64) for g in range(PASSES)]
         w8 = [keep.tile([P, D * 4], U8, name="w8_%d" % g, align_bytes=64) for g in range(W8_PASSES)]
         w4 = keep.tile([P, W4_PASSES, D * 2], U8, name="w4", align_bytes=64)
-        w8_plane = keep.tile([P, W8_PASSES * D], U8, name="w8_plane", align_bytes=64)
-        w4_plane = keep.tile([P, W4_PASSES * D], U8, name="w4_plane", align_bytes=64)
+        w_plane = keep.tile([P, PASSES * D], U8, name="w_plane", align_bytes=64)
         result = [keep.tile([P, D], F32, name="result%d" % b, align_bytes=64) for b in range(TILES)]
         acc = [
-            [(d0, d1, psum.tile([P, d1 - d0], F32, name="acc%d_%d" % (b, d0))) for d0, d1 in spans]
-            for b, spans in enumerate(((0, H), (H, D)) if b in HALVED else ((0, D),) for b in range(TILES))
+            [(d0, d1, psum.tile([P, d1 - d0], F32, name="acc%d_%d" % (b, d0))) for d0, d1 in zip(cuts, cuts[1:])]
+            for b, cuts in enumerate(CUTS)
         ]
 
-        nc.vector.memset(w4_plane[:].bitcast(I32), 0)
-        nc.vector.memset(w8_plane[:].bitcast(I32), 0)
+        nc.vector.memset(w_plane[:].bitcast(I32), 0)
 
         def load_whole(g):
             nc.sync.dma_start(out=raw[g][:], in_=dy_rows[g])
 
-        nc.sync.dma_start(
-            out=first_raw[:].rearrange("p g j t -> p g (j t)"),
-            in_=dy_rows[2:4].rearrange("g p j t -> p g (j t)"),
-        )
-        load_scales(nc, w4_plane, w4_scales, W4_PASSES)
         nc.sync.dma_start(out=early_raw[:], in_=dy_rows[SPLIT][:, :, 0:EARLY])
+        land_scales(nc, w_plane, w4_scales, W8_PASSES, PASSES)
+        land_scales(nc, w_plane, w8_scales, 0, W8_PASSES)
         nc.sync.dma_start(
             out=w4[:].rearrange("p a b -> p (a b)").bitcast(I32).rearrange("p (a b) -> p a b", a=W4_PASSES),
             in_=w4_words.rearrange("a p b -> p a b").bitcast(I32),
         )
-        load_scales(nc, w8_plane, w8_scales, W8_PASSES)
-        load_whole(4)
-        load_whole(0)
+        load_whole(2)
+        move_scales(nc, w_plane)
+        for g in (3, 4, 0):
+            load_whole(g)
         for g in (1, 0):
             nc.sync.dma_start(
                 out=w8[g][:].bitcast(I32), in_=w8_words[g].rearrange("p d i -> p (d i)").bitcast(I32)
@@ -114,17 +108,14 @@ def tile_mix_dyq_tm_none_kernel(tc, dy, w8_words, w8_scales, w4_words, w4_scales
             for d0, d1, bank in acc[b]:
                 if g < W8_PASSES:
                     words = w8[g][:, 4 * d0 : 4 * d1].bitcast(E4M3X4)
-                    plane = w8_plane[:, g * D + d0 : g * D + d1]
                 else:
-                    a = g - W8_PASSES
-                    words = w4[:, a, 2 * d0 : 2 * d1].bitcast(E2M1X4)
-                    plane = w4_plane[:, a * D + d0 : a * D + d1]
+                    words = w4[:, g - W8_PASSES, 2 * d0 : 2 * d1].bitcast(E2M1X4)
                 nc.tensor.matmul_mx(
                     out=bank[:],
                     lhsT=codes[g][:, cols].bitcast(E5M2X4),
                     lhsT_scale=scales[g][:, cols],
                     rhs=words,
-                    rhs_scale=plane,
+                    rhs_scale=w_plane[:, g * D + d0 : g * D + d1],
                     start=(g == W8_PASSES),
                     stop=stop,
                 )
@@ -134,15 +125,13 @@ def tile_mix_dyq_tm_none_kernel(tc, dy, w8_words, w8_scales, w4_words, w4_scales
                 copy(out=result[b][:, d0:d1], in_=bank[:])
             nc.sync.dma_start(out=out[b * P : (b + 1) * P, :], in_=result[b][:])
 
-        prepare_whole(2)
-        prepare_whole(3)
         interleave(nc.scalar.copy, grouped[SPLIT], early_raw, V_EARLY, EARLY)
         interleave(nc.vector.tensor_copy, grouped[SPLIT], early_raw, 0, P)
         interleave(nc.vector.tensor_copy, grouped[SPLIT], early_raw, P, V_EARLY)
         quantise(SPLIT, 0, P)
         quantise(SPLIT, P, EARLY)
-        prepare_whole(4)
-        prepare_whole(0)
+        for g in (2, 3, 4, 0):
+            prepare_whole(g)
 
         for g in range(W8_PASSES, PASSES):
             for b in range(TILES):
@@ -155,9 +144,8 @@ def tile_mix_dyq_tm_none_kernel(tc, dy, w8_words, w8_scales, w4_words, w4_scales
         multiply(0, 2, stop=True)
         multiply(0, 3)
 
-        finish(0, nc.vector.tensor_copy, nc.scalar.copy)
+        finish(0, nc.scalar.copy, nc.vector.tensor_copy, nc.vector.tensor_copy)
         finish(1, nc.scalar.copy)
-        finish(2, nc.scalar.copy)
 
         halves = ((EARLY, EARLY + P // 2), (EARLY + P // 2, T))
         for t0, t1 in halves:
@@ -165,4 +153,5 @@ def tile_mix_dyq_tm_none_kernel(tc, dy, w8_words, w8_scales, w4_words, w4_scales
         for t0, t1 in halves:
             quantise(SPLIT, t0, t1)
         multiply(SPLIT, 3, stop=True)
+        finish(2, nc.scalar.copy, nc.vector.tensor_copy)
         finish(3, nc.vector.tensor_copy, nc.scalar.copy)

@@ -52,16 +52,16 @@ def tile_mix_dyq_tm_none_kernel(tc, dy, w8_words, w8_scales, w4_words, w4_scales
         psum = ctx.enter_context(tc.psum_pool(name="psum", bufs=1))
         ctx.enter_context(tc.manual_schedule())
 
-        raw = {g: keep.tile([P, J, T], F32, name="raw%d" % g, align_bytes=64) for g in range(PASSES) if g != SPLIT}
-        early_raw = keep.tile([P, J, EARLY], F32, name="early_raw", align_bytes=64)
-        late_raw = keep.tile([P, J, P], F32, name="late_raw", align_bytes=64)
-        grouped = [keep.tile([P, T, J], BF16, name="grouped%d" % g, align_bytes=64) for g in range(PASSES)]
-        codes = [keep.tile([P, T], U32, name="codes%d" % g, align_bytes=64) for g in range(PASSES)]
-        scales = [keep.tile([P, T], U8, name="scales%d" % g, align_bytes=64) for g in range(PASSES)]
-        w8 = [keep.tile([P, D * 4], U8, name="w8_%d" % g, align_bytes=64) for g in range(W8_PASSES)]
-        w4 = keep.tile([P, W4_PASSES, D * 2], U8, name="w4", align_bytes=64)
-        w_plane = keep.tile([P, PASSES * D], U8, name="w_plane", align_bytes=64)
-        result = [keep.tile([P, D], F32, name="result%d" % b, align_bytes=64) for b in range(TILES)]
+        raw = {g: keep.tile([P, J, T], F32, name="raw%d" % g, align_bytes=256) for g in range(PASSES) if g != SPLIT}
+        early_raw = keep.tile([P, J, EARLY], F32, name="early_raw", align_bytes=256)
+        late_raw = keep.tile([P, J, P], F32, name="late_raw", align_bytes=256)
+        grouped = [keep.tile([P, T, J], BF16, name="grouped%d" % g, align_bytes=256) for g in range(PASSES)]
+        codes = [keep.tile([P, T], U32, name="codes%d" % g, align_bytes=256) for g in range(PASSES)]
+        scales = [keep.tile([P, T], U8, name="scales%d" % g, align_bytes=256) for g in range(PASSES)]
+        w8 = [keep.tile([P, D * 4], U8, name="w8_%d" % g, align_bytes=256) for g in range(W8_PASSES)]
+        w4 = keep.tile([P, W4_PASSES, D * 2], U8, name="w4", align_bytes=256)
+        w_plane = keep.tile([P, PASSES * D], U8, name="w_plane", align_bytes=256)
+        result = [keep.tile([P, D], F32, name="result%d" % b, align_bytes=256) for b in range(TILES)]
         acc = [
             [(d0, d1, psum.tile([P, d1 - d0], F32, name="acc%d_%d" % (b, d0))) for d0, d1 in zip(cuts, cuts[1:])]
             for b, cuts in enumerate(CUTS)

@@ -20,20 +20,12 @@ PASSES = 5
 W8_PASSES = 2
 W4_PASSES = 3
 TILES = 4
-SPLIT = 1
+LAST = TILES - 1
 EARLY = T - P
-CUTS = ((0, D // 2, 3 * D // 4, D), (0, D), (0, D // 2, D), (0, D // 2, D))
+ALIGN = 256
+LATE = (4, 1, 0)
+CUTS = ((0, D // 2, D), (0, D), (0, D), (0, D // 4, D // 2, 3 * D // 4, D))
 V_EARLY = 208
-
-
-def land_scales(nc, plane, scales, g0, g1):
-    words = plane[:].bitcast(I32).rearrange("p (a d) -> p a d", a=PASSES)
-    nc.sync.dma_start(out=words[0:P:8, g0:g1, :], in_=scales.bitcast(I32).rearrange("a q d -> q a d"))
-
-
-def move_scales(nc, plane):
-    for r in range(1, 4):
-        nc.sync.dma_start(out=plane[r:P:32, :].bitcast(I32), in_=plane[8 * r : P : 32, :].bitcast(I32))
 
 
 def interleave(copy, grouped, raw, t0, t1, base=0):
@@ -52,16 +44,18 @@ def tile_mix_dyq_tm_none_kernel(tc, dy, w8_words, w8_scales, w4_words, w4_scales
         psum = ctx.enter_context(tc.psum_pool(name="psum", bufs=1))
         ctx.enter_context(tc.manual_schedule())
 
-        raw = {g: keep.tile([P, J, T], F32, name="raw%d" % g, align_bytes=256) for g in range(PASSES) if g != SPLIT}
-        early_raw = keep.tile([P, J, EARLY], F32, name="early_raw", align_bytes=256)
-        late_raw = keep.tile([P, J, P], F32, name="late_raw", align_bytes=256)
-        grouped = [keep.tile([P, T, J], BF16, name="grouped%d" % g, align_bytes=256) for g in range(PASSES)]
-        codes = [keep.tile([P, T], U32, name="codes%d" % g, align_bytes=256) for g in range(PASSES)]
-        scales = [keep.tile([P, T], U8, name="scales%d" % g, align_bytes=256) for g in range(PASSES)]
-        w8 = [keep.tile([P, D * 4], U8, name="w8_%d" % g, align_bytes=256) for g in range(W8_PASSES)]
-        w4 = keep.tile([P, W4_PASSES, D * 2], U8, name="w4", align_bytes=256)
-        w_plane = keep.tile([P, PASSES * D], U8, name="w_plane", align_bytes=256)
-        result = [keep.tile([P, D], F32, name="result%d" % b, align_bytes=256) for b in range(TILES)]
+        def sbuf(name, shape, dtype):
+            return keep.tile(shape, dtype, name=name, align_bytes=ALIGN)
+
+        raw = [sbuf("raw%d" % g, [P, J, EARLY if g in LATE else T], F32) for g in range(PASSES)]
+        late_raw = {g: sbuf("late_raw%d" % g, [P, J, P], F32) for g in LATE}
+        grouped = [sbuf("grouped%d" % g, [P, T, J], BF16) for g in range(PASSES)]
+        codes = [sbuf("codes%d" % g, [P, T], U32) for g in range(PASSES)]
+        scales = [sbuf("scales%d" % g, [P, T], U8) for g in range(PASSES)]
+        w8 = [sbuf("w8_%d" % g, [P, D * 4], U8) for g in range(W8_PASSES)]
+        w4 = sbuf("w4", [P, W4_PASSES, D * 2], U8)
+        w_plane = sbuf("w_plane", [P, PASSES * D], U8)
+        result = [sbuf("result%d" % b, [P, D], F32) for b in range(TILES)]
         acc = [
             [(d0, d1, psum.tile([P, d1 - d0], F32, name="acc%d_%d" % (b, d0))) for d0, d1 in zip(cuts, cuts[1:])]
             for b, cuts in enumerate(CUTS)
@@ -69,25 +63,26 @@ def tile_mix_dyq_tm_none_kernel(tc, dy, w8_words, w8_scales, w4_words, w4_scales
 
         nc.vector.memset(w_plane[:].bitcast(I32), 0)
 
-        def load_whole(g):
-            nc.sync.dma_start(out=raw[g][:], in_=dy_rows[g])
+        def load(g):
+            nc.sync.dma_start(out=raw[g][:], in_=dy_rows[g][:, :, 0 : EARLY if g in LATE else T])
 
-        nc.sync.dma_start(out=early_raw[:], in_=dy_rows[SPLIT][:, :, 0:EARLY])
-        land_scales(nc, w_plane, w4_scales, W8_PASSES, PASSES)
-        land_scales(nc, w_plane, w8_scales, 0, W8_PASSES)
+        plane_words = w_plane[:].bitcast(I32).rearrange("p (a d) -> p a d", a=PASSES)
+        load(1)
+        for rows, g0, g1 in ((w4_scales, W8_PASSES, PASSES), (w8_scales, 0, W8_PASSES)):
+            nc.sync.dma_start(out=plane_words[0:P:8, g0:g1, :], in_=rows.bitcast(I32).rearrange("a q d -> q a d"))
         nc.sync.dma_start(
             out=w4[:].rearrange("p a b -> p (a b)").bitcast(I32).rearrange("p (a b) -> p a b", a=W4_PASSES),
             in_=w4_words.rearrange("a p b -> p a b").bitcast(I32),
         )
-        load_whole(2)
-        move_scales(nc, w_plane)
+        load(2)
+        for r in range(1, 4):
+            nc.sync.dma_start(out=w_plane[r:P:32, :].bitcast(I32), in_=w_plane[8 * r : P : 32, :].bitcast(I32))
         for g in (3, 4, 0):
-            load_whole(g)
+            load(g)
         for g in (1, 0):
-            nc.sync.dma_start(
-                out=w8[g][:].bitcast(I32), in_=w8_words[g].rearrange("p d i -> p (d i)").bitcast(I32)
-            )
-        nc.sync.dma_start(out=late_raw[:], in_=dy_rows[SPLIT][:, :, EARLY:T])
+            nc.sync.dma_start(out=w8[g][:].bitcast(I32), in_=w8_words[g].rearrange("p d i -> p (d i)").bitcast(I32))
+        for g in LATE:
+            nc.sync.dma_start(out=late_raw[g][:], in_=dy_rows[g][:, :, EARLY:T])
 
         def quantise(g, t0, t1):
             nc.vector.quantize_mx(
@@ -96,12 +91,19 @@ def tile_mix_dyq_tm_none_kernel(tc, dy, w8_words, w8_scales, w4_words, w4_scales
                 in_=grouped[g][:, t0:t1, :].rearrange("p t j -> p (t j)"),
             )
 
-        def prepare_whole(g):
-            for b in range(TILES):
-                copy = nc.vector.tensor_copy if b < TILES // 2 else nc.scalar.copy
-                interleave(copy, grouped[g], raw[g], b * P, (b + 1) * P)
-            for b in range(TILES):
-                quantise(g, b * P, (b + 1) * P)
+        def prepare(g):
+            if g in LATE:
+                interleave(nc.scalar.copy, grouped[g], raw[g], V_EARLY, EARLY)
+                interleave(nc.vector.tensor_copy, grouped[g], raw[g], 0, P)
+                interleave(nc.vector.tensor_copy, grouped[g], raw[g], P, V_EARLY)
+                quantise(g, 0, P)
+                quantise(g, P, EARLY)
+            else:
+                for b in range(TILES):
+                    copy = nc.vector.tensor_copy if b < TILES // 2 else nc.scalar.copy
+                    interleave(copy, grouped[g], raw[g], b * P, (b + 1) * P)
+                for b in range(TILES):
+                    quantise(g, b * P, (b + 1) * P)
 
         def multiply(g, b, stop=False):
             cols = slice(b * P, (b + 1) * P)
@@ -120,21 +122,17 @@ def tile_mix_dyq_tm_none_kernel(tc, dy, w8_words, w8_scales, w4_words, w4_scales
                     stop=stop,
                 )
 
-        def finish(b, *copies):
-            for copy, (d0, d1, bank) in zip(copies, acc[b]):
+        def empty(b, parts, copies):
+            for copy, (d0, d1, bank) in zip(copies, parts):
                 copy(out=result[b][:, d0:d1], in_=bank[:])
-            nc.sync.dma_start(out=out[b * P : (b + 1) * P, :], in_=result[b][:])
+            d0, d1 = parts[0][0], parts[-1][1]
+            nc.sync.dma_start(out=out[b * P : (b + 1) * P, d0:d1], in_=result[b][:, d0:d1])
 
-        interleave(nc.scalar.copy, grouped[SPLIT], early_raw, V_EARLY, EARLY)
-        interleave(nc.vector.tensor_copy, grouped[SPLIT], early_raw, 0, P)
-        interleave(nc.vector.tensor_copy, grouped[SPLIT], early_raw, P, V_EARLY)
-        quantise(SPLIT, 0, P)
-        quantise(SPLIT, P, EARLY)
-        for g in (2, 3, 4, 0):
-            prepare_whole(g)
+        for g in (1, 2, 3, 4, 0):
+            prepare(g)
 
         for g in range(W8_PASSES, PASSES):
-            for b in range(TILES):
+            for b in range(LAST if g in LATE else TILES):
                 multiply(g, b)
         multiply(1, 0)
         multiply(1, 1)
@@ -142,16 +140,22 @@ def tile_mix_dyq_tm_none_kernel(tc, dy, w8_words, w8_scales, w4_words, w4_scales
         multiply(0, 1, stop=True)
         multiply(1, 2)
         multiply(0, 2, stop=True)
-        multiply(0, 3)
 
-        finish(0, nc.scalar.copy, nc.vector.tensor_copy, nc.vector.tensor_copy)
-        finish(1, nc.scalar.copy)
+        empty(0, acc[0], (nc.scalar.copy, nc.vector.tensor_copy))
+        empty(1, acc[1], (nc.scalar.copy,))
 
-        halves = ((EARLY, EARLY + P // 2), (EARLY + P // 2, T))
-        for t0, t1 in halves:
-            interleave(nc.vector.tensor_copy, grouped[SPLIT], late_raw, t0, t1, EARLY)
-        for t0, t1 in halves:
-            quantise(SPLIT, t0, t1)
-        multiply(SPLIT, 3, stop=True)
-        finish(2, nc.scalar.copy, nc.vector.tensor_copy)
-        finish(3, nc.vector.tensor_copy, nc.scalar.copy)
+        first, second, third = LATE
+        middle = EARLY + P // 2
+        interleave(nc.vector.tensor_copy, grouped[first], late_raw[first], EARLY, T, EARLY)
+        interleave(nc.vector.tensor_copy, grouped[second], late_raw[second], EARLY, T, EARLY)
+        quantise(first, EARLY, T)
+        interleave(nc.vector.tensor_copy, grouped[third], late_raw[third], EARLY, middle, EARLY)
+        interleave(nc.scalar.copy, grouped[third], late_raw[third], middle, T, EARLY)
+        empty(2, acc[2], (nc.scalar.copy,))
+        quantise(second, EARLY, T)
+        quantise(third, middle, T)
+        quantise(third, EARLY, middle)
+        for g in LATE:
+            multiply(g, LAST, stop=(g == third))
+        empty(LAST, acc[LAST][0:2], (nc.vector.tensor_copy, nc.scalar.copy))
+        empty(LAST, acc[LAST][2:4], (nc.vector.tensor_copy, nc.scalar.copy))

@@ -23,7 +23,7 @@ TILES = 4
 LAST = TILES - 1
 EARLY = T - P
 ALIGN = 256
-LATE = (4, 1, 0)
+LATE = (3, 4, 1, 0)
 CUTS = ((0, D // 2, D), (0, D), (0, D), (0, D // 4, D // 2, 3 * D // 4, D))
 V_EARLY = 208
 
@@ -144,18 +144,24 @@ def tile_mix_dyq_tm_none_kernel(tc, dy, w8_words, w8_scales, w4_words, w4_scales
         empty(0, acc[0], (nc.scalar.copy, nc.vector.tensor_copy))
         empty(1, acc[1], (nc.scalar.copy,))
 
-        first, second, third = LATE
-        middle = EARLY + P // 2
-        interleave(nc.vector.tensor_copy, grouped[first], late_raw[first], EARLY, T, EARLY)
-        interleave(nc.vector.tensor_copy, grouped[second], late_raw[second], EARLY, T, EARLY)
-        quantise(first, EARLY, T)
-        interleave(nc.vector.tensor_copy, grouped[third], late_raw[third], EARLY, middle, EARLY)
-        interleave(nc.scalar.copy, grouped[third], late_raw[third], middle, T, EARLY)
         empty(2, acc[2], (nc.scalar.copy,))
-        quantise(second, EARLY, T)
-        quantise(third, middle, T)
-        quantise(third, EARLY, middle)
+
+        middle = EARLY + P // 2
+
+        def lay_late(g, shared):
+            if shared:
+                interleave(nc.vector.tensor_copy, grouped[g], late_raw[g], EARLY, middle, EARLY)
+                interleave(nc.scalar.copy, grouped[g], late_raw[g], middle, T, EARLY)
+            else:
+                interleave(nc.vector.tensor_copy, grouped[g], late_raw[g], EARLY, T, EARLY)
+
+        lay_late(LATE[0], False)
+        for before, g in zip(LATE, LATE[1:]):
+            lay_late(g, g == LATE[-1])
+            quantise(before, EARLY, T)
+        quantise(LATE[-1], middle, T)
+        quantise(LATE[-1], EARLY, middle)
         for g in LATE:
-            multiply(g, LAST, stop=(g == third))
+            multiply(g, LAST, stop=(g == LATE[-1]))
         empty(LAST, acc[LAST][0:2], (nc.vector.tensor_copy, nc.scalar.copy))
         empty(LAST, acc[LAST][2:4], (nc.vector.tensor_copy, nc.scalar.copy))

from contextlib import ExitStack

import concourse.mybir as mybir

K, T, D = 2560, 512, 512
FLOPS = 2 * K * T * D

F32 = mybir.dt.float32
BF16 = mybir.dt.bfloat16
I32 = mybir.dt.int32
U32 = mybir.dt.uint32
U8 = mybir.dt.uint8
E5M2X4 = mybir.dt.float8_e5m2_x4
E4M3X4 = mybir.dt.float8_e4m3fn_x4
E2M1X4 = mybir.dt.float4_e2m1fn_x4

P = 128
J = 4
PASSES = 5
W8_PASSES = 2
W4_PASSES = 3
TILES = 4
LAST = TILES - 1
EARLY = T - P
ALIGN = 256
LATE = (3, 4, 1, 0)
CUTS = ((0, D // 2, D), (0, D), (0, D), (0, D // 4, D // 2, 3 * D // 4, D))
V_EARLY = 208


def interleave(copy, grouped, raw, t0, t1, base=0):
    copy(
        out=grouped[:, t0:t1, :].rearrange("p (c i) j -> p c j i", i=4),
        in_=raw[:, :, t0 - base : t1 - base].rearrange("p j (c i) -> p c j i", i=4),
    )


def tile_mix_dyq_tm_none_kernel(tc, dy, w8_words, w8_scales, w4_words, w4_scales, out):
    nc = tc.nc
    dy_rows = dy.rearrange("(g p j) t -> g p j t", p=P, j=J)

    with ExitStack() as ctx:
        keep = ctx.enter_context(tc.tile_pool(name="keep", bufs=1))
        psum = ctx.enter_context(tc.psum_pool(name="psum", bufs=1))
        ctx.enter_context(tc.manual_schedule())

        def sbuf(name, shape, dtype):
            return keep.tile(shape, dtype, name=name, align_bytes=ALIGN)

        raw = [sbuf("raw%d" % g, [P, J, EARLY if g in LATE else T], F32) for g in range(PASSES)]
        late_raw = {g: sbuf("late_raw%d" % g, [P, J, P], F32) for g in LATE}
        grouped = [sbuf("grouped%d" % g, [P, T, J], BF16) for g in range(PASSES)]
        codes = [sbuf("codes%d" % g, [P, T], U32) for g in range(PASSES)]
        scales = [sbuf("scales%d" % g, [P, T], U8) for g in range(PASSES)]
        w8 = [sbuf("w8_%d" % g, [P, D * 4], U8) for g in range(W8_PASSES)]
        w4 = sbuf("w4", [P, W4_PASSES, D * 2], U8)
        w_plane = sbuf("w_plane", [P, PASSES * D], U8)
        result = [sbuf("result%d" % b, [P, D], F32) for b in range(TILES)]
        acc = [
            [(d0, d1, psum.tile([P, d1 - d0], F32, name="acc%d_%d" % (b, d0))) for d0, d1 in zip(cuts, cuts[1:])]
            for b, cuts in enumerate(CUTS)
        ]

        nc.vector.memset(w_plane[:].bitcast(I32), 0)

        def load(g):
            nc.sync.dma_start(out=raw[g][:], in_=dy_rows[g][:, :, 0 : EARLY if g in LATE else T])

        plane_words = w_plane[:].bitcast(I32).rearrange("p (a d) -> p a d", a=PASSES)
        load(1)
        for rows, g0, g1 in ((w4_scales, W8_PASSES, PASSES), (w8_scales, 0, W8_PASSES)):
            nc.sync.dma_start(out=plane_words[0:P:8, g0:g1, :], in_=rows.bitcast(I32).rearrange("a q d -> q a d"))
        nc.sync.dma_start(
            out=w4[:].rearrange("p a b -> p (a b)").bitcast(I32).rearrange("p (a b) -> p a b", a=W4_PASSES),
            in_=w4_words.rearrange("a p b -> p a b").bitcast(I32),
        )
        load(2)
        for r in range(1, 4):
            nc.sync.dma_start(out=w_plane[r:P:32, :].bitcast(I32), in_=w_plane[8 * r : P : 32, :].bitcast(I32))
        for g in (3, 4, 0):
            load(g)
        for g in (1, 0):
            nc.sync.dma_start(out=w8[g][:].bitcast(I32), in_=w8_words[g].rearrange("p d i -> p (d i)").bitcast(I32))
        for g in LATE:
            nc.sync.dma_start(out=late_raw[g][:], in_=dy_rows[g][:, :, EARLY:T])

        def quantise(g, t0, t1):
            nc.vector.quantize_mx(
                out=codes[g][:, t0:t1].bitcast(E5M2X4),
                scales=scales[g][:, t0:t1],
                in_=grouped[g][:, t0:t1, :].rearrange("p t j -> p (t j)"),
            )

        def prepare(g):
            if g in LATE:
                interleave(nc.scalar.copy, grouped[g], raw[g], V_EARLY, EARLY)
                interleave(nc.vector.tensor_copy, grouped[g], raw[g], 0, P)
                interleave(nc.vector.tensor_copy, grouped[g], raw[g], P, V_EARLY)
                quantise(g, 0, P)
                quantise(g, P, EARLY)
            else:
                for b in range(TILES):
                    copy = nc.vector.tensor_copy if b < TILES // 2 else nc.scalar.copy
                    interleave(copy, grouped[g], raw[g], b * P, (b + 1) * P)
                for b in range(TILES):
                    quantise(g, b * P, (b + 1) * P)

        def multiply(g, b, stop=False):
            cols = slice(b * P, (b + 1) * P)
            for d0, d1, bank in acc[b]:
                if g < W8_PASSES:
                    words = w8[g][:, 4 * d0 : 4 * d1].bitcast(E4M3X4)
                else:
                    words = w4[:, g - W8_PASSES, 2 * d0 : 2 * d1].bitcast(E2M1X4)
                nc.tensor.matmul_mx(
                    out=bank[:],
                    lhsT=codes[g][:, cols].bitcast(E5M2X4),
                    lhsT_scale=scales[g][:, cols],
                    rhs=words,
                    rhs_scale=w_plane[:, g * D + d0 : g * D + d1],
                    start=(g == W8_PASSES),
                    stop=stop,
                )

        def empty(b, parts, copies):
            for copy, (d0, d1, bank) in zip(copies, parts):
                copy(out=result[b][:, d0:d1], in_=bank[:])
            d0, d1 = parts[0][0], parts[-1][1]
            nc.sync.dma_start(out=out[b * P : (b + 1) * P, d0:d1], in_=result[b][:, d0:d1])

        for g in (1, 2, 3, 4, 0):
            prepare(g)

        for g in range(W8_PASSES, PASSES):
            for b in range(LAST if g in LATE else TILES):
                multiply(g, b)
        multiply(1, 0)
        multiply(1, 1)
        multiply(0, 0, stop=True)
        multiply(0, 1, stop=True)
        multiply(1, 2)
        multiply(0, 2, stop=True)

        empty(0, acc[0], (nc.scalar.copy, nc.vector.tensor_copy))
        empty(1, acc[1], (nc.scalar.copy,))

        empty(2, acc[2], (nc.scalar.copy,))

        middle = EARLY + P // 2

        def lay_late(g, shared):
            if shared:
                interleave(nc.vector.tensor_copy, grouped[g], late_raw[g], EARLY, middle, EARLY)
                interleave(nc.scalar.copy, grouped[g], late_raw[g], middle, T, EARLY)
            else:
                interleave(nc.vector.tensor_copy, grouped[g], late_raw[g], EARLY, T, EARLY)

        lay_late(LATE[0], False)
        for before, g in zip(LATE, LATE[1:]):
            lay_late(g, g == LATE[-1])
            quantise(before, EARLY, T)
        quantise(LATE[-1], middle, T)
        quantise(LATE[-1], EARLY, middle)
        for g in LATE:
            multiply(g, LAST, stop=(g == LATE[-1]))
        empty(LAST, acc[LAST][0:2], (nc.vector.tensor_copy, nc.scalar.copy))
        empty(LAST, acc[LAST][2:4], (nc.vector.tensor_copy, nc.scalar.copy))
